import numpy as np
import ml_dtypes


def mxq(x, axis, fmt="e4m3"):
    dtype, down = {"e4m3": (ml_dtypes.float8_e4m3fn, 7), "e5m2": (ml_dtypes.float8_e5m2, 14)}[fmt]
    v = np.moveaxis(np.asarray(x, np.float32).astype(ml_dtypes.bfloat16).astype(np.float64), axis, -1)
    blocks = v.reshape(v.shape[:-1] + (-1, 32))
    amax = np.abs(blocks).max(-1, keepdims=True)
    byte = np.maximum(np.where(amax > 0, np.frexp(amax)[1] - 1 + 127, 0) - down, 1)
    scale = np.exp2(byte - 127.0)
    codes = (blocks / scale).astype(np.float32).astype(dtype).astype(np.float64)
    return np.moveaxis((codes * scale).reshape(v.shape), -1, axis)


WIDE = False


def mx_kscale(k):
    if not WIDE:
        return np.ones(k)
    levels = np.array([10, -10, 5, -5, 0])
    if k % 512:
        return np.exp2(np.random.permutation(np.resize(levels, k // 32))).repeat(32)
    a = np.empty((k // 512, 16))
    for p in range(k // 512):
        a[p, :8] = np.random.permutation(np.resize(levels, 8))
        for g in range(8):
            far = levels[np.abs(levels - a[p, g]) >= 10]
            a[p, g + 8] = far[np.random.randint(len(far))]
    return np.exp2(a.ravel()).repeat(32)


def f64(x):
    return np.asarray(x).astype(np.float64)


def striped(idx):
    return np.tile(idx.reshape(-1, 16).T, (8, 1)).astype(np.uint16)


def unstriped(offs):
    return offs[:16].T.reshape(-1).astype(np.int64)


def pack_weight(w):
    k, n = w.shape
    w = f64(np.asarray(w, np.float32).astype(ml_dtypes.bfloat16)).reshape(k // 32, 32, n)
    amax = np.abs(w).max(1)
    byte = np.clip(np.where(amax > 0, np.frexp(amax)[1] - 1 + 127 - 7, 1), 1, 254)
    scaled = (w * np.exp2(127.0 - byte)[:, None, :]).reshape(k, n).astype(np.float32)
    words = np.ascontiguousarray(scaled.reshape(k // 512, 128, 4, n).transpose(0, 1, 3, 2)).astype(ml_dtypes.float8_e4m3fn).view(np.uint8)
    return words, np.ascontiguousarray(byte.astype(np.uint8).reshape(k // 512, 16, n))


def unpack_weight(words, scales):
    g, p, n, _ = words.shape
    vals = np.ascontiguousarray(words).view(ml_dtypes.float8_e4m3fn).astype(np.float64) * np.repeat(np.exp2(scales.astype(np.float64) - 127.0), 8, axis=1)[..., None]
    return vals.transpose(0, 1, 3, 2).reshape(g * 512, n)


def sigmoid(v):
    return 1.0 / (1.0 + np.exp(-np.maximum(v, -700.0)))


K, T, S, V = 512, 2048, 512, 512


def setup_inputs():
    n = np.random.standard_normal
    s = mx_kscale(K)[:, None]
    packed_xT = pack_weight(n((K, T)) * s)
    packed_eT = pack_weight(n((K, T)) * s)
    packed_dT = pack_weight(n((K, T)) * s)
    return {
        "x_words": packed_xT[0],
        "x_scales": packed_xT[1],
        "e_words": packed_eT[0],
        "e_scales": packed_eT[1],
        "d_words": packed_dT[0],
        "d_scales": packed_dT[1],
        "hT": (n((K, V)) / np.sqrt(K) / s).astype(np.float32),
        "gT": (n((K, V)) / np.sqrt(K) / s).astype(np.float32),
        "fT": (n((K, V)) / np.sqrt(K) / s).astype(np.float32),
        "offs": striped(np.random.permutation(T)[:S]),
    }


def reference(x_words, x_scales, e_words, e_scales, d_words, d_scales, hT, gT, fT, offs):
    gTq = mxq(f64(gT), 0, "e4m3")
    e_offs = unpack_weight(e_words, e_scales)[:, unstriped(offs)]
    z = gTq.T @ e_offs
    fTq = mxq(f64(fT), 0, "e4m3")
    d_offs = unpack_weight(d_words, d_scales)[:, unstriped(offs)]
    gg = sigmoid(fTq.T @ d_offs)
    hTq = mxq(f64(hT), 0, "e4m3")
    xq = unpack_weight(x_words, x_scales)[:, unstriped(offs)]
    y = hTq.T @ xq
    return z + gg * (y - z)

@@ -1,0 +1,166 @@
+from contextlib import ExitStack
+
+import concourse.mybir as mybir
+
+K, T, S, V = 512, 2048, 512, 512
+FLOPS = 3 * 2 * K * V * S
+
+F32 = mybir.dt.float32
+BF16 = mybir.dt.bfloat16
+I32 = mybir.dt.int32
+U32 = mybir.dt.uint32
+U16 = mybir.dt.uint16
+U8 = mybir.dt.uint8
+FP8X4 = mybir.dt.float8_e4m3fn_x4
+ACT = mybir.ActivationFunctionType
+ALU = mybir.AluOpType
+
+P = 128
+PACK = 4
+M = 128
+
+
+def tile_picked_ymol_mol_p_kernel(
+    tc, x_words, x_scales, e_words, e_scales, d_words, d_scales, hT, gT, fT, offs, out
+):
+    nc = tc.nc
+    with ExitStack() as ctx:
+        keep = ctx.enter_context(tc.tile_pool(name="keep", bufs=1))
+        psum = ctx.enter_context(tc.psum_pool(name="psum", bufs=1))
+
+        offsets = keep.tile([P, S // 16], U16, name="offsets")
+
+        def load_words(name, words):
+            table = keep.tile([P, T], I32, name=name + "_word_table", align_bytes=64)
+            nc.sync.dma_start(out=table[:], in_=words[0].rearrange("p n t -> p (n t)").bitcast(I32))
+            return table
+
+        def clear_scales(name):
+            table = keep.tile([P, T], U8, name=name + "_scale_table", align_bytes=64)
+            nc.vector.memset(table[:].bitcast(I32), 0)
+            return table
+
+        def load_scales(table, scales, first_row, queue):
+            rows = scales[0].bitcast(I32).rearrange("(q r) c -> r q c", r=4)
+            for r in range(4):
+                queue.dma_start(out=table[first_row + r : P : 32, :].bitcast(I32), in_=rows[r])
+
+        def gather_words(name, table):
+            picked = keep.tile([P, S], U32, name=name + "_words", align_bytes=64)
+            nc.vector.tensor_copy(picked[:], table[:].bitcast(U32).indirect(offsets[:]))
+            return picked
+
+        def gather_scales(name, table):
+            picked = keep.tile([P, S], U8, name=name + "_scales", align_bytes=64)
+            nc.vector.tensor_copy(picked[:], table[:].indirect(offsets[:]))
+            return picked
+
+        def load_users(name, matrix, c0, c1):
+            raw = keep.tile([P, PACK, c1 - c0], F32, name=name + "_raw", align_bytes=64)
+            nc.sync.dma_start(out=raw[:], in_=matrix[:, c0:c1].rearrange("(p j) w -> p j w", j=PACK))
+            return raw
+
+        def cast(name, raw, a, b, negate=False, engine="scalar"):
+            grouped = keep.tile([P, b - a, PACK], BF16, name=name + "_bf16", align_bytes=64)
+            dst = grouped[:].rearrange("p (c i) j -> p c j i", i=4)
+            src = raw[:, :, a:b].rearrange("p j (c i) -> p c j i", i=4)
+            if negate:
+                nc.scalar.activation(dst, src, ACT.Copy, scale=-1.0)
+            elif engine == "scalar":
+                nc.scalar.copy(dst, src)
+            else:
+                nc.vector.tensor_copy(dst, src)
+            return grouped
+
+        def quantize(name, grouped):
+            width = grouped.shape[1]
+            codes = keep.tile([P, width], U32, name=name + "_codes", align_bytes=64)
+            scales = keep.tile([P, width], U8, name=name + "_cscales", align_bytes=64)
+            nc.vector.quantize_mx(
+                out=codes[:].bitcast(FP8X4), scales=scales[:], in_=grouped[:].rearrange("p w j -> p (w j)")
+            )
+            return [(codes[:, m : m + M], scales[:, m : m + M]) for m in range(0, width, M)]
+
+        def product(acc, users, items, start=True, stop=True):
+            words, scales, first_row = items
+            nc.tensor.matmul_mx(
+                out=acc[:],
+                lhsT=users[0].bitcast(FP8X4),
+                lhsT_scale=users[1],
+                rhs=words[:].bitcast(FP8X4),
+                rhs_scale=scales[first_row:P, :],
+                start=start,
+                stop=stop,
+            )
+
+        def bank(name, b):
+            return psum.tile([P, S], F32, name=name, tag="bank%d" % b)
+
+        def gate(i, fq, items):
+            u = bank("u%d" % i, i)
+            product(u, fq, items)
+            gg = keep.tile([P, S], F32, name="gg%d" % i)
+            nc.scalar.activation(gg[:], u[:], ACT.Sigmoid)
+            return gg
+
+        def z_part(i, gg, nz):
+            zpart = keep.tile([P, S], F32, name="zpart%d" % i)
+            nc.vector.scalar_tensor_tensor(zpart[:], gg[:], 1.0, nz[:], ALU.subtract, ALU.mult)
+            return zpart
+
+        def scaled(i, gg, y, a=0, b=S):
+            part = keep.tile([P, b - a], F32, name="ypart%d_%d" % (i, a))
+            nc.vector.tensor_tensor(part[:], y[:, a:b], gg[:, a:b], ALU.mult)
+            return part
+
+        def finish(i, part, other, op, engine, a=0, b=S, queue=nc.sync):
+            res = keep.tile([P, b - a], F32, name="res%d_%d" % (i, a))
+            engine.tensor_tensor(res[:], part[:], other[:, a:b], op)
+            queue.dma_start(out=out[i * M : (i + 1) * M, a:b], in_=res[:])
+
+        d_st = clear_scales("d")
+        e_st = clear_scales("e")
+        x_st = clear_scales("x")
+        nc.sync.dma_start(out=offsets[:], in_=offs)
+        f_raw = load_users("f", fT, 0, V)
+        load_scales(d_st, d_scales, 0, nc.sync)
+        g_raw = load_users("g", gT, 0, V)
+        load_scales(e_st, e_scales, 4, nc.sync)
+        d_wt = load_words("d", d_words)
+        load_scales(x_st, x_scales, 8, nc.sync)
+        e_wt = load_words("e", e_words)
+        x_wt = load_words("x", x_words)
+        h01_raw = load_users("h01", hT, 0, 256)
+        h23_raw = load_users("h23", hT, 256, 512)
+
+        fq = quantize("f01", cast("f01", f_raw, 0, 256)) + quantize("f23", cast("f23", f_raw, 256, 512))
+        d_s = gather_scales("d", d_st)
+        gq = quantize("g01", cast("g01", g_raw, 0, 256, negate=True)) + quantize("g23", cast("g23", g_raw, 256, 512, negate=True))
+        e_s = gather_scales("e", e_st)
+        d_items = (gather_words("d", d_wt), d_s, 0)
+        gg = [gate(i, fq[i], d_items) for i in range(4)]
+        x_s = gather_scales("x", x_st)
+        e_items = (gather_words("e", e_wt), e_s, 4)
+        x_items = (gather_words("x", x_wt), x_s, 8)
+        hq = []
+        for i in range(4):
+            hq = hq + quantize("h%d" % i, cast("h%d" % i, (h01_raw, h23_raw)[i // 2], (i % 2) * M, (i % 2 + 1) * M))
+        nz, y, zp = [], [], []
+        for i in range(4):
+            nz.append(bank("nz%d" % i, 4 + i))
+            y.append(bank("y%d" % i, i))
+            if i < 2:
+                product(nz[i], gq[i], e_items)
+                zp.append(z_part(i, gg[i], nz[i]))
+                product(y[i], hq[i], x_items)
+            else:
+                product(y[i], gq[i], e_items, True, False)
+                product(y[i], hq[i], x_items, False, True)
+                product(nz[i], gq[i], e_items)
+        for i in range(2):
+            finish(i, scaled(i, gg[i], y[i]), zp[i], ALU.add, nc.gpsimd)
+        finish(2, scaled(2, gg[2], y[2]), nz[2], ALU.subtract, nc.vector)
+        p3a = scaled(3, gg[3], y[3], 0, 256)
+        p3b = scaled(3, gg[3], y[3], 256, 512)
+        finish(3, p3a, nz[3], ALU.subtract, nc.vector, 0, 256)
+        finish(3, p3b, nz[3], ALU.subtract, nc.vector, 256, 512)

@@ -121,13 +121,13 @@ def tile_picked_ymol_mol_p_kernel(
         d_st = clear_scales("d")
         e_st = clear_scales("e")
         x_st = clear_scales("x")
-        nc.sync.dma_start(out=offsets[:], in_=offs)
         f_raw = load_users("f", fT, 0, V)
+        nc.sync.dma_start(out=offsets[:], in_=offs)
         load_scales(d_st, d_scales, 0, nc.sync)
         g_raw = load_users("g", gT, 0, V)
-        load_scales(e_st, e_scales, 4, nc.sync)
+        load_scales(e_st, e_scales, 4, nc.gpsimd)
         d_wt = load_words("d", d_words)
-        load_scales(x_st, x_scales, 8, nc.sync)
+        load_scales(x_st, x_scales, 8, nc.gpsimd)
         e_wt = load_words("e", e_words)
         x_wt = load_words("x", x_words)
         h01_raw = load_users("h01", hT, 0, 256)

@@ -17,7 +17,12 @@ ALU = mybir.AluOpType
 
 P = 128
 PACK = 4
+BLOCK_PARTITIONS = 8
+QUADRANT = 32
 M = 128
+TILES = V // M
+HALF = V // 2
+LINE = 4
 
 
 def tile_picked_ymol_mol_p_kernel(
@@ -25,142 +30,137 @@ def tile_picked_ymol_mol_p_kernel(
 ):
     nc = tc.nc
     with ExitStack() as ctx:
-        keep = ctx.enter_context(tc.tile_pool(name="keep", bufs=1))
+        sbuf = ctx.enter_context(tc.tile_pool(name="sbuf", bufs=1))
         psum = ctx.enter_context(tc.psum_pool(name="psum", bufs=1))
 
-        offsets = keep.tile([P, S // 16], U16, name="offsets")
-
-        def load_words(name, words):
-            table = keep.tile([P, T], I32, name=name + "_word_table", align_bytes=64)
-            nc.sync.dma_start(out=table[:], in_=words[0].rearrange("p n t -> p (n t)").bitcast(I32))
-            return table
-
-        def clear_scales(name):
-            table = keep.tile([P, T], U8, name=name + "_scale_table", align_bytes=64)
+        def zeroed_scale_table(name):
+            table = sbuf.tile([P, T], U8, name=name + "_scale_table", align_bytes=64)
             nc.vector.memset(table[:].bitcast(I32), 0)
             return table
 
-        def load_scales(table, scales, first_row, queue):
-            rows = scales[0].bitcast(I32).rearrange("(q r) c -> r q c", r=4)
-            for r in range(4):
-                queue.dma_start(out=table[first_row + r : P : 32, :].bitcast(I32), in_=rows[r])
+        def load_word_table(name, words):
+            table = sbuf.tile([P, T], I32, name=name + "_word_table", align_bytes=64)
+            nc.sync.dma_start(out=table[:], in_=words[0].rearrange("p n t -> p (n t)").bitcast(I32))
+            return table
+
+        def load_users(name, matrix, first, count):
+            raw = sbuf.tile([P, PACK, count], F32, name=name + "_raw", align_bytes=64)
+            columns = matrix[:, first : first + count]
+            nc.sync.dma_start(out=raw[:], in_=columns.rearrange("(p j) u -> p j u", j=PACK))
+            return raw
 
         def gather_words(name, table):
-            picked = keep.tile([P, S], U32, name=name + "_words", align_bytes=64)
+            picked = sbuf.tile([P, S], U32, name=name + "_words", align_bytes=64)
             nc.vector.tensor_copy(picked[:], table[:].bitcast(U32).indirect(offsets[:]))
             return picked
 
-        def gather_scales(name, table):
-            picked = keep.tile([P, S], U8, name=name + "_scales", align_bytes=64)
-            nc.vector.tensor_copy(picked[:], table[:].indirect(offsets[:]))
-            return picked
-
-        def load_users(name, matrix, c0, c1):
-            raw = keep.tile([P, PACK, c1 - c0], F32, name=name + "_raw", align_bytes=64)
-            nc.sync.dma_start(out=raw[:], in_=matrix[:, c0:c1].rearrange("(p j) w -> p j w", j=PACK))
-            return raw
-
-        def cast(name, raw, a, b, negate=False, engine="scalar"):
-            grouped = keep.tile([P, b - a, PACK], BF16, name=name + "_bf16", align_bytes=64)
-            dst = grouped[:].rearrange("p (c i) j -> p c j i", i=4)
-            src = raw[:, :, a:b].rearrange("p j (c i) -> p c j i", i=4)
+        def quantize_users(name, raw, negate=False):
+            count = raw.shape[2]
+            rounded = sbuf.tile([P, count, PACK], BF16, name=name + "_bf16", align_bytes=64)
+            dst = rounded[:].rearrange("p (c i) j -> p c j i", i=LINE)
+            src = raw.rearrange("p j (c i) -> p c j i", i=LINE)
             if negate:
                 nc.scalar.activation(dst, src, ACT.Copy, scale=-1.0)
-            elif engine == "scalar":
-                nc.scalar.copy(dst, src)
             else:
-                nc.vector.tensor_copy(dst, src)
-            return grouped
-
-        def quantize(name, grouped):
-            width = grouped.shape[1]
-            codes = keep.tile([P, width], U32, name=name + "_codes", align_bytes=64)
-            scales = keep.tile([P, width], U8, name=name + "_cscales", align_bytes=64)
+                nc.scalar.copy(dst, src)
+            codes = sbuf.tile([P, count], U32, name=name + "_codes", align_bytes=64)
+            scales = sbuf.tile([P, count], U8, name=name + "_scales", align_bytes=64)
             nc.vector.quantize_mx(
-                out=codes[:].bitcast(FP8X4), scales=scales[:], in_=grouped[:].rearrange("p w j -> p (w j)")
+                out=codes[:].bitcast(FP8X4), scales=scales[:], in_=rounded[:].rearrange("p u j -> p (u j)")
             )
-            return [(codes[:, m : m + M], scales[:, m : m + M]) for m in range(0, width, M)]
+            return [(codes[:, m : m + M], scales[:, m : m + M]) for m in range(0, count, M)]
 
         def product(acc, users, items, start=True, stop=True):
-            words, scales, first_row = items
             nc.tensor.matmul_mx(
                 out=acc[:],
                 lhsT=users[0].bitcast(FP8X4),
                 lhsT_scale=users[1],
-                rhs=words[:].bitcast(FP8X4),
-                rhs_scale=scales[first_row:P, :],
+                rhs=items[0][:].bitcast(FP8X4),
+                rhs_scale=items[1],
                 start=start,
                 stop=stop,
             )
 
-        def bank(name, b):
-            return psum.tile([P, S], F32, name=name, tag="bank%d" % b)
+        def bank(name, number):
+            return psum.tile([P, S], F32, name=name, tag="bank%d" % number)
 
-        def gate(i, fq, items):
-            u = bank("u%d" % i, i)
-            product(u, fq, items)
-            gg = keep.tile([P, S], F32, name="gg%d" % i)
-            nc.scalar.activation(gg[:], u[:], ACT.Sigmoid)
-            return gg
+        def times_gate(i, acc, first, count):
+            gated = sbuf.tile([P, count], F32, name="gated%d_%d" % (i, first))
+            columns = slice(first, first + count)
+            nc.vector.tensor_tensor(gated[:], acc[:, columns], gates[i][:, columns], ALU.mult)
+            return gated
 
-        def z_part(i, gg, nz):
-            zpart = keep.tile([P, S], F32, name="zpart%d" % i)
-            nc.vector.scalar_tensor_tensor(zpart[:], gg[:], 1.0, nz[:], ALU.subtract, ALU.mult)
-            return zpart
+        def combine_and_store(i, gated, other, op, first, count):
+            result = sbuf.tile([P, count], F32, name="result%d_%d" % (i, first))
+            columns = slice(first, first + count)
+            nc.vector.tensor_tensor(result[:], gated[:], other[:, columns], op)
+            nc.sync.dma_start(out=out[i * M : (i + 1) * M, columns], in_=result[:])
 
-        def scaled(i, gg, y, a=0, b=S):
-            part = keep.tile([P, b - a], F32, name="ypart%d_%d" % (i, a))
-            nc.vector.tensor_tensor(part[:], y[:, a:b], gg[:, a:b], ALU.mult)
-            return part
-
-        def finish(i, part, other, op, engine, a=0, b=S, queue=nc.sync):
-            res = keep.tile([P, b - a], F32, name="res%d_%d" % (i, a))
-            engine.tensor_tensor(res[:], part[:], other[:, a:b], op)
-            queue.dma_start(out=out[i * M : (i + 1) * M, a:b], in_=res[:])
-
-        d_st = clear_scales("d")
-        e_st = clear_scales("e")
-        x_st = clear_scales("x")
-        f_raw = load_users("f", fT, 0, V)
+        scale_inputs = (("d", d_scales), ("e", e_scales), ("x", x_scales))
+        scale_tables = [zeroed_scale_table(name) for name, scales in scale_inputs]
+        g_first = load_users("g_first", gT, 0, HALF)
+        offsets = sbuf.tile([P, S // 16], U16, name="offsets")
         nc.sync.dma_start(out=offsets[:], in_=offs)
-        load_scales(d_st, d_scales, 0, nc.sync)
-        g_raw = load_users("g", gT, 0, V)
-        load_scales(e_st, e_scales, 4, nc.gpsimd)
-        d_wt = load_words("d", d_words)
-        load_scales(x_st, x_scales, 8, nc.gpsimd)
-        e_wt = load_words("e", e_words)
-        x_wt = load_words("x", x_words)
-        h01_raw = load_users("h01", hT, 0, 256)
-        h23_raw = load_users("h23", hT, 256, 512)
+        for table, (name, scales) in zip(scale_tables, scale_inputs):
+            nc.sync.dma_start(out=table[0:P:BLOCK_PARTITIONS, :].bitcast(I32), in_=scales[0].bitcast(I32))
+        f_raw = load_users("f", fT, 0, V)
+        d_table = load_word_table("d", d_words)
+        e_table = load_word_table("e", e_words)
 
-        fq = quantize("f01", cast("f01", f_raw, 0, 256)) + quantize("f23", cast("f23", f_raw, 256, 512))
-        d_s = gather_scales("d", d_st)
-        gq = quantize("g01", cast("g01", g_raw, 0, 256, negate=True)) + quantize("g23", cast("g23", g_raw, 256, 512, negate=True))
-        e_s = gather_scales("e", e_st)
-        d_items = (gather_words("d", d_wt), d_s, 0)
-        gg = [gate(i, fq[i], d_items) for i in range(4)]
-        x_s = gather_scales("x", x_st)
-        e_items = (gather_words("e", e_wt), e_s, 4)
-        x_items = (gather_words("x", x_wt), x_s, 8)
-        hq = []
-        for i in range(4):
-            hq = hq + quantize("h%d" % i, cast("h%d" % i, (h01_raw, h23_raw)[i // 2], (i % 2) * M, (i % 2 + 1) * M))
-        nz, y, zp = [], [], []
-        for i in range(4):
-            nz.append(bank("nz%d" % i, 4 + i))
-            y.append(bank("y%d" % i, i))
-            if i < 2:
-                product(nz[i], gq[i], e_items)
-                zp.append(z_part(i, gg[i], nz[i]))
-                product(y[i], hq[i], x_items)
-            else:
-                product(y[i], gq[i], e_items, True, False)
-                product(y[i], hq[i], x_items, False, True)
-                product(nz[i], gq[i], e_items)
-        for i in range(2):
-            finish(i, scaled(i, gg[i], y[i]), zp[i], ALU.add, nc.gpsimd)
-        finish(2, scaled(2, gg[2], y[2]), nz[2], ALU.subtract, nc.vector)
-        p3a = scaled(3, gg[3], y[3], 0, 256)
-        p3b = scaled(3, gg[3], y[3], 256, 512)
-        finish(3, p3a, nz[3], ALU.subtract, nc.vector, 0, 256)
-        finish(3, p3b, nz[3], ALU.subtract, nc.vector, 256, 512)
+        picked_scales = sbuf.tile([P, len(scale_tables) * S], U8, name="picked_scales", align_bytes=64)
+        for t, table in enumerate(scale_tables):
+            nc.vector.tensor_copy(picked_scales[:, t * S : (t + 1) * S], table[:].indirect(offsets[:]))
+        item_scales = sbuf.tile([P, len(scale_tables) * S], U8, name="item_scales", align_bytes=64)
+        nc.vector.tensor_copy(item_scales[:].bitcast(I32), picked_scales[:].bitcast(I32))
+        for r in range(1, QUADRANT // BLOCK_PARTITIONS):
+            nc.sync.dma_start(
+                out=item_scales[r:P:QUADRANT, :].bitcast(I32),
+                in_=picked_scales[BLOCK_PARTITIONS * r : P : QUADRANT, :].bitcast(I32),
+            )
+        x_table = load_word_table("x", x_words)
+
+        neg_g = quantize_users("g_first", g_first[:], negate=True)
+        f_codes = []
+        for first in range(0, V, HALF):
+            f_codes.extend(quantize_users("f%d" % first, f_raw[:, :, first : first + HALF]))
+        d_items = (gather_words("d", d_table), item_scales[:, 0:S])
+
+        late = []
+        for i in range(TILES):
+            if i * M >= HALF:
+                late.append(("g%d" % i, load_users("g%d" % i, gT, i * M, M), True))
+            late.append(("h%d" % i, load_users("h%d" % i, hT, i * M, M), False))
+        e_items = (gather_words("e", e_table), item_scales[:, S : 2 * S])
+        x_items = (gather_words("x", x_table), item_scales[:, 2 * S : 3 * S])
+        h_codes = []
+        for name, raw, is_g in late:
+            (neg_g if is_g else h_codes).extend(quantize_users(name, raw[:], negate=is_g))
+
+        gates = []
+        for i in range(TILES):
+            logits = bank("logits%d" % i, i)
+            product(logits, f_codes[i], d_items)
+            gate = sbuf.tile([P, S], F32, name="gate%d" % i)
+            nc.scalar.activation(gate[:], logits[:], ACT.Sigmoid)
+            gates.append(gate)
+
+        neg_z = [bank("neg_z%d" % i, TILES + i) for i in range(TILES)]
+        product(neg_z[0], neg_g[0], e_items)
+        z_share = sbuf.tile([P, S], F32, name="z_share")
+        nc.vector.scalar_tensor_tensor(z_share[:], gates[0][:], 1.0, neg_z[0][:], ALU.subtract, ALU.mult)
+        y_first = bank("y0", 0)
+        product(y_first, h_codes[0], x_items)
+        y_minus_z = {}
+        for i in range(1, TILES):
+            y_minus_z[i] = bank("y_minus_z%d" % i, i)
+            product(y_minus_z[i], neg_g[i], e_items, start=True, stop=False)
+            product(y_minus_z[i], h_codes[i], x_items, start=False, stop=True)
+            product(neg_z[i], neg_g[i], e_items)
+
+        combine_and_store(0, times_gate(0, y_first, 0, S), z_share, ALU.add, 0, S)
+        for i in range(1, TILES - 1):
+            combine_and_store(i, times_gate(i, y_minus_z[i], 0, S), neg_z[i], ALU.subtract, 0, S)
+        last = TILES - 1
+        halves = [(first, times_gate(last, y_minus_z[last], first, S // 2)) for first in (0, S // 2)]
+        for first, gated in halves:
+            combine_and_store(last, gated, neg_z[last], ALU.subtract, first, S // 2)

from contextlib import ExitStack

import concourse.mybir as mybir

K, T, S, V = 512, 2048, 512, 512
FLOPS = 3 * 2 * K * V * S

F32 = mybir.dt.float32
BF16 = mybir.dt.bfloat16
I32 = mybir.dt.int32
U32 = mybir.dt.uint32
U16 = mybir.dt.uint16
U8 = mybir.dt.uint8
FP8X4 = mybir.dt.float8_e4m3fn_x4
ACT = mybir.ActivationFunctionType
ALU = mybir.AluOpType

P = 128
PACK = 4
BLOCK_PARTITIONS = 8
QUADRANT = 32
M = 128
TILES = V // M
HALF = V // 2
LINE = 4


def tile_picked_ymol_mol_p_kernel(
    tc, x_words, x_scales, e_words, e_scales, d_words, d_scales, hT, gT, fT, offs, out
):
    nc = tc.nc
    with ExitStack() as ctx:
        sbuf = ctx.enter_context(tc.tile_pool(name="sbuf", bufs=1))
        psum = ctx.enter_context(tc.psum_pool(name="psum", bufs=1))

        def zeroed_scale_table(name):
            table = sbuf.tile([P, T], U8, name=name + "_scale_table", align_bytes=64)
            nc.vector.memset(table[:].bitcast(I32), 0)
            return table

        def load_word_table(name, words):
            table = sbuf.tile([P, T], I32, name=name + "_word_table", align_bytes=64)
            nc.sync.dma_start(out=table[:], in_=words[0].rearrange("p n t -> p (n t)").bitcast(I32))
            return table

        def load_users(name, matrix, first, count):
            raw = sbuf.tile([P, PACK, count], F32, name=name + "_raw", align_bytes=64)
            columns = matrix[:, first : first + count]
            nc.sync.dma_start(out=raw[:], in_=columns.rearrange("(p j) u -> p j u", j=PACK))
            return raw

        def gather_words(name, table):
            picked = sbuf.tile([P, S], U32, name=name + "_words", align_bytes=64)
            nc.vector.tensor_copy(picked[:], table[:].bitcast(U32).indirect(offsets[:]))
            return picked

        def quantize_users(name, raw, negate=False):
            count = raw.shape[2]
            rounded = sbuf.tile([P, count, PACK], BF16, name=name + "_bf16", align_bytes=64)
            dst = rounded[:].rearrange("p (c i) j -> p c j i", i=LINE)
            src = raw.rearrange("p j (c i) -> p c j i", i=LINE)
            if negate:
                nc.scalar.activation(dst, src, ACT.Copy, scale=-1.0)
            else:
                nc.scalar.copy(dst, src)
            codes = sbuf.tile([P, count], U32, name=name + "_codes", align_bytes=64)
            scales = sbuf.tile([P, count], U8, name=name + "_scales", align_bytes=64)
            nc.vector.quantize_mx(
                out=codes[:].bitcast(FP8X4), scales=scales[:], in_=rounded[:].rearrange("p u j -> p (u j)")
            )
            return [(codes[:, m : m + M], scales[:, m : m + M]) for m in range(0, count, M)]

        def product(acc, users, items, start=True, stop=True):
            nc.tensor.matmul_mx(
                out=acc[:],
                lhsT=users[0].bitcast(FP8X4),
                lhsT_scale=users[1],
                rhs=items[0][:].bitcast(FP8X4),
                rhs_scale=items[1],
                start=start,
                stop=stop,
            )

        def bank(name, number):
            return psum.tile([P, S], F32, name=name, tag="bank%d" % number)

        def times_gate(i, acc, first, count):
            gated = sbuf.tile([P, count], F32, name="gated%d_%d" % (i, first))
            columns = slice(first, first + count)
            nc.vector.tensor_tensor(gated[:], acc[:, columns], gates[i][:, columns], ALU.mult)
            return gated

        def combine_and_store(i, gated, other, op, first, count):
            result = sbuf.tile([P, count], F32, name="result%d_%d" % (i, first))
            columns = slice(first, first + count)
            nc.vector.tensor_tensor(result[:], gated[:], other[:, columns], op)
            nc.sync.dma_start(out=out[i * M : (i + 1) * M, columns], in_=result[:])

        scale_inputs = (("d", d_scales), ("e", e_scales), ("x", x_scales))
        scale_tables = [zeroed_scale_table(name) for name, scales in scale_inputs]
        g_first = load_users("g_first", gT, 0, HALF)
        offsets = sbuf.tile([P, S // 16], U16, name="offsets")
        nc.sync.dma_start(out=offsets[:], in_=offs)
        for table, (name, scales) in zip(scale_tables, scale_inputs):
            nc.sync.dma_start(out=table[0:P:BLOCK_PARTITIONS, :].bitcast(I32), in_=scales[0].bitcast(I32))
        f_raw = load_users("f", fT, 0, V)
        d_table = load_word_table("d", d_words)
        e_table = load_word_table("e", e_words)

        picked_scales = sbuf.tile([P, len(scale_tables) * S], U8, name="picked_scales", align_bytes=64)
        for t, table in enumerate(scale_tables):
            nc.vector.tensor_copy(picked_scales[:, t * S : (t + 1) * S], table[:].indirect(offsets[:]))
        item_scales = sbuf.tile([P, len(scale_tables) * S], U8, name="item_scales", align_bytes=64)
        nc.vector.tensor_copy(item_scales[:].bitcast(I32), picked_scales[:].bitcast(I32))
        for r in range(1, QUADRANT // BLOCK_PARTITIONS):
            nc.sync.dma_start(
                out=item_scales[r:P:QUADRANT, :].bitcast(I32),
                in_=picked_scales[BLOCK_PARTITIONS * r : P : QUADRANT, :].bitcast(I32),
            )
        x_table = load_word_table("x", x_words)

        neg_g = quantize_users("g_first", g_first[:], negate=True)
        f_codes = []
        for first in range(0, V, HALF):
            f_codes.extend(quantize_users("f%d" % first, f_raw[:, :, first : first + HALF]))
        d_items = (gather_words("d", d_table), item_scales[:, 0:S])

        late = []
        for i in range(TILES):
            if i * M >= HALF:
                late.append(("g%d" % i, load_users("g%d" % i, gT, i * M, M), True))
            late.append(("h%d" % i, load_users("h%d" % i, hT, i * M, M), False))
        e_items = (gather_words("e", e_table), item_scales[:, S : 2 * S])
        x_items = (gather_words("x", x_table), item_scales[:, 2 * S : 3 * S])
        h_codes = []
        for name, raw, is_g in late:
            (neg_g if is_g else h_codes).extend(quantize_users(name, raw[:], negate=is_g))

        gates = []
        for i in range(TILES):
            logits = bank("logits%d" % i, i)
            product(logits, f_codes[i], d_items)
            gate = sbuf.tile([P, S], F32, name="gate%d" % i)
            nc.scalar.activation(gate[:], logits[:], ACT.Sigmoid)
            gates.append(gate)

        neg_z = [bank("neg_z%d" % i, TILES + i) for i in range(TILES)]
        product(neg_z[0], neg_g[0], e_items)
        z_share = sbuf.tile([P, S], F32, name="z_share")
        nc.vector.scalar_tensor_tensor(z_share[:], gates[0][:], 1.0, neg_z[0][:], ALU.subtract, ALU.mult)
        y_first = bank("y0", 0)
        product(y_first, h_codes[0], x_items)
        y_minus_z = {}
        for i in range(1, TILES):
            y_minus_z[i] = bank("y_minus_z%d" % i, i)
            product(y_minus_z[i], neg_g[i], e_items, start=True, stop=False)
            product(y_minus_z[i], h_codes[i], x_items, start=False, stop=True)
            product(neg_z[i], neg_g[i], e_items)

        combine_and_store(0, times_gate(0, y_first, 0, S), z_share, ALU.add, 0, S)
        for i in range(1, TILES - 1):
            combine_and_store(i, times_gate(i, y_minus_z[i], 0, S), neg_z[i], ALU.subtract, 0, S)
        last = TILES - 1
        halves = [(first, times_gate(last, y_minus_z[last], first, S // 2)) for first in (0, S // 2)]
        for first, gated in halves:
            combine_and_store(last, gated, neg_z[last], ALU.subtract, first, S // 2)
